import numpy as np
import ml_dtypes


def mxq(x, axis, fmt="e4m3"):
    dtype, down = {"e4m3": (ml_dtypes.float8_e4m3fn, 7), "e5m2": (ml_dtypes.float8_e5m2, 14)}[fmt]
    v = np.moveaxis(np.asarray(x, np.float32).astype(ml_dtypes.bfloat16).astype(np.float64), axis, -1)
    blocks = v.reshape(v.shape[:-1] + (-1, 32))
    amax = np.abs(blocks).max(-1, keepdims=True)
    byte = np.maximum(np.where(amax > 0, np.frexp(amax)[1] - 1 + 127, 0) - down, 1)
    scale = np.exp2(byte - 127.0)
    codes = (blocks / scale).astype(np.float32).astype(dtype).astype(np.float64)
    return np.moveaxis((codes * scale).reshape(v.shape), -1, axis)


WIDE = False


def mx_kscale(k):
    if not WIDE:
        return np.ones(k)
    levels = np.array([10, -10, 5, -5, 0])
    if k % 512:
        return np.exp2(np.random.permutation(np.resize(levels, k // 32))).repeat(32)
    a = np.empty((k // 512, 16))
    for p in range(k // 512):
        a[p, :8] = np.random.permutation(np.resize(levels, 8))
        for g in range(8):
            far = levels[np.abs(levels - a[p, g]) >= 10]
            a[p, g + 8] = far[np.random.randint(len(far))]
    return np.exp2(a.ravel()).repeat(32)


def f64(x):
    return np.asarray(x).astype(np.float64)


def striped8(idx):
    return np.concatenate([v.reshape(-1, 16).T for v in idx]).astype(np.uint16)


def unstriped8(offs):
    return np.stack([offs[16 * g:16 * g + 16].T.reshape(-1) for g in range(8)]).astype(np.int64)


E2M1 = np.array([0.0, 0.5, 1.0, 1.5, 2.0, 3.0, 4.0, 6.0, -0.0, -0.5, -1.0, -1.5, -2.0, -3.0, -4.0, -6.0])


def pack_weight(w, fmt):
    k, n = w.shape
    w = f64(np.asarray(w, np.float32).astype(ml_dtypes.bfloat16)).reshape(k // 32, 32, n)
    amax = np.abs(w).max(1)
    if fmt == "e4m3":
        byte = np.frexp(amax)[1] - 1 + 127 - 7
    else:
        mant, ex = np.frexp(amax / 6.0)
        byte = np.where(mant > 0.5, ex, ex - 1) + 127
    byte = np.clip(np.where(amax > 0, byte, 1), 1, 254)
    scaled = (w * np.exp2(127.0 - byte)[:, None, :]).reshape(k, n).astype(np.float32)
    by_word = np.ascontiguousarray(scaled.reshape(k // 512, 128, 4, n).transpose(0, 1, 3, 2))
    if fmt == "e4m3":
        words = by_word.astype(ml_dtypes.float8_e4m3fn).view(np.uint8)
    else:
        c = by_word.astype(ml_dtypes.float4_e2m1fn).view(np.uint8) & 0xF
        words = (c[..., 0::2] | (c[..., 1::2] << 4)).reshape(k // 512, 128, 2 * n)
    return np.ascontiguousarray(words), np.ascontiguousarray(byte.astype(np.uint8).reshape(k // 512, 16, n))


def unpack_weight(words, scales, fmt):
    g, _, n = scales.shape
    words = np.ascontiguousarray(words).reshape(g, 128, n, -1)
    if fmt == "e4m3":
        vals = words.view(ml_dtypes.float8_e4m3fn).astype(np.float64)
    else:
        nib = np.empty((g, 128, n, 4), np.uint8)
        nib[..., 0::2] = words & 0xF
        nib[..., 1::2] = words >> 4
        vals = E2M1[nib]
    vals = vals * np.repeat(np.exp2(scales.astype(np.float64) - 127.0), 8, axis=1)[..., None]
    return vals.transpose(0, 1, 3, 2).reshape(g * 512, n)


K, M, T, S = 1536, 512, 1024, 512


def setup_inputs():
    n = np.random.standard_normal
    s = mx_kscale(K)[:, None]
    p_w = pack_weight(n((K, M)) / np.sqrt(K) / s, "e2m1")
    return {
        "xT": (n((K, T)) * s).astype(np.float32),
        "w_words": p_w[0],
        "w_scales": p_w[1],
        "wgt": np.repeat(np.random.uniform(0.5, 2.0, (8, S)), 16, axis=0).astype(np.float32),
        "b": (0.3 * n(512)).astype(np.float32),
        "offs": striped8(np.stack([np.random.permutation(T)[:S] for _ in range(8)])),
    }


def reference(xT, w_words, w_scales, wgt, b, offs):
    idx = unstriped8(offs)
    group = np.arange(K) % 512 // 64
    xg = f64(wgt)[np.arange(K) // 4 % 128] * f64(xT)[np.arange(K)[:, None], idx[group]]
    xT_ = mxq(xg, 0, "e4m3")
    w_ = unpack_weight(w_words, w_scales, "e2m1")
    y = w_.T @ xT_
    return y + f64(b)[:, None]

@@ -1,0 +1,186 @@
+from contextlib import ExitStack
+
+import concourse.mybir as mybir
+
+K, M, T, S = 1536, 512, 1024, 512
+FLOPS = 2 * K * M * S
+
+F32 = mybir.dt.float32
+BF16 = mybir.dt.bfloat16
+I32 = mybir.dt.int32
+U32 = mybir.dt.uint32
+U16 = mybir.dt.uint16
+U8 = mybir.dt.uint8
+FP8X4 = mybir.dt.float8_e4m3fn_x4
+FP4X4 = mybir.dt.float4_e2m1fn_x4
+MULT = mybir.AluOpType.mult
+ADD = mybir.AluOpType.add
+IDENTITY = mybir.ActivationFunctionType.Identity
+
+P = 128
+PACK = 4
+K_PASS = P * PACK
+PASSES = K // K_PASS
+LANES = 16
+CHUNK = 128
+HALF = 256
+N_TILES = M // P
+BIAS_PAD = 8
+
+
+def tile_list_heads_bias_kernel(tc, xT, w_words, w_scales, wgt, b, offs, out):
+    nc = tc.nc
+    with ExitStack() as ctx:
+        keep = ctx.enter_context(tc.tile_pool(name="keep", bufs=1))
+        psum = ctx.enter_context(tc.psum_pool(name="psum", bufs=1))
+
+        offsets = keep.tile([P, S // LANES], U16, name="offsets")
+        weights = keep.tile([P, S], F32, name="weights")
+        planes = [
+            [keep.tile([P, T], F32, name="plane_%d_%d" % (a, i)) for i in range(PACK)] for a in range(PASSES)
+        ]
+        picked = [keep.tile([P, PACK, S], F32, name="picked_%d" % a) for a in range(PASSES)]
+        grouped = [keep.tile([P, S, PACK], BF16, name="grouped_%d" % a, align_bytes=64) for a in range(PASSES)]
+        x_codes = keep.tile([P, PASSES, S], U32, name="x_codes", align_bytes=64)
+        x_scales = keep.tile([P, PASSES, S], U8, name="x_scales", align_bytes=64)
+        w_codes = keep.tile([P, PASSES, 2 * M], U8, name="w_codes", align_bytes=64)
+        w_scale_rows = keep.tile([P, PASSES, M], U8, name="w_scale_rows", align_bytes=64)
+        bias = keep.tile([P, N_TILES, BIAS_PAD], F32, name="bias")
+        result = keep.tile([P, S // HALF, N_TILES, HALF], F32, name="result")
+        primer_in = keep.tile([P, 1], F32, name="primer_in")
+        primer_out = keep.tile([P, 1], F32, name="primer_out")
+        banks = [
+            [psum.tile([P, HALF], F32, name="bank_%d_%d" % (h, n)) for n in range(N_TILES)] for h in range(S // HALF)
+        ]
+
+        nc.vector.memset(primer_in[:], 0.0)
+        nc.scalar.activation(primer_out[:], primer_in[:], IDENTITY, bias=primer_in[:])
+        nc.vector.memset(w_scale_rows[:].bitcast(I32), 0)
+
+        def load_plane(a, i):
+            rows = xT[a * K_PASS : (a + 1) * K_PASS, :].rearrange("(p i) t -> p i t", i=PACK)
+            nc.sync.dma_start(planes[a][i][:], rows[:, i, :])
+
+        def load_w(a):
+            nc.sync.dma_start(w_codes[:, a, :].bitcast(I32), w_words[a].bitcast(I32))
+
+        def load_w_scales():
+            for q in range(4):
+                nc.sync.dma_start(
+                    w_scale_rows[32 * q : 32 * q + 4, :, :].bitcast(I32),
+                    w_scales[:, 4 * q : 4 * q + 4, :].rearrange("a r n -> r a n").bitcast(I32),
+                )
+
+        load_plane(0, 0)
+        nc.sync.dma_start(offsets[:], offs)
+        nc.sync.dma_start(weights[:], wgt)
+        for i in (1, 2, 3):
+            load_plane(0, i)
+        for i in (0, 1):
+            load_plane(1, i)
+        load_w_scales()
+        for i in (2, 3):
+            load_plane(1, i)
+        load_w(0)
+        for i in (0, 1, 2):
+            load_plane(2, i)
+        load_w(1)
+        load_plane(2, 3)
+        load_w(2)
+        with nc.allow_non_contiguous_dma(reason="one bias value to a partition"):
+            nc.sync.dma_start(bias[:, :, 0], b.rearrange("(n p) -> p n", p=P))
+
+        def gather(a, i, lo, hi):
+            window = planes[a][i][:].indirect(offsets[:, lo // LANES : hi // LANES])
+            nc.vector.tensor_tensor(picked[a][:, i, lo:hi], window, weights[:, lo:hi], MULT)
+
+        def interleave_views(a, lo, hi):
+            dst = grouped[a][:, lo:hi, :].rearrange("p (c e) i -> p c i e", e=4)
+            src = picked[a][:, :, lo:hi].rearrange("p i (c e) -> p c i e", e=4)
+            return dst, src
+
+        def interleave(a, lo, hi):
+            nc.scalar.copy(*interleave_views(a, lo, hi))
+
+        def quantize(a, lo, hi):
+            nc.vector.quantize_mx(
+                out=x_codes[:, a, lo:hi].bitcast(FP8X4),
+                scales=x_scales[:, a, lo:hi],
+                in_=grouped[a][:, lo:hi, :].rearrange("p j i -> p (j i)"),
+            )
+
+        def multiply(a, c):
+            h, side = divmod(c, 2)
+            cols = slice(c * CHUNK, (c + 1) * CHUNK)
+            for n in range(N_TILES):
+                nc.tensor.matmul_mx(
+                    out=banks[h][n][:, side * CHUNK : (side + 1) * CHUNK],
+                    lhsT=w_codes[:, a, 2 * P * n : 2 * P * (n + 1)].bitcast(FP4X4),
+                    lhsT_scale=w_scale_rows[:, a, P * n : P * (n + 1)],
+                    rhs=x_codes[:, a, cols].bitcast(FP8X4),
+                    rhs_scale=x_scales[:, a, cols],
+                    start=(a == 0 and side == 0),
+                    stop=(a == PASSES - 1 and side == 1),
+                )
+
+        def store(h, n):
+            nc.sync.dma_start(out[P * n : P * (n + 1), HALF * h : HALF * (h + 1)], result[:, h, n, :])
+
+        def finish_on_scalar(h, n):
+            nc.scalar.activation(result[:, h, n, :], banks[h][n][:], IDENTITY, bias=bias[:, n, 0:1])
+            store(h, n)
+
+        def finish_on_vector(h, n):
+            nc.vector.tensor_scalar(result[:, h, n, :], banks[h][n][:], bias[:, n, 0:1], None, ADD)
+            store(h, n)
+
+        def gather_in_halves(a, i):
+            gather(a, i, 0, HALF)
+            gather(a, i, HALF, S)
+
+        for i in range(PACK):
+            gather_in_halves(0, i)
+        interleave(0, 0, HALF)
+        interleave(0, HALF, S)
+        gather_in_halves(1, 0)
+        gather_in_halves(1, 1)
+        quantize(0, 0, S)
+        gather_in_halves(1, 2)
+        gather_in_halves(1, 3)
+        for c in range(4):
+            multiply(0, c)
+        interleave(1, 0, HALF)
+        interleave(1, HALF, S)
+
+        last = PASSES - 1
+        tail = S - CHUNK
+        gather(last, 0, 0, tail)
+        gather(last, 1, 0, tail)
+        quantize(1, 0, HALF)
+        gather(last, 2, 0, tail)
+        quantize(1, HALF, S)
+        for c in range(4):
+            multiply(1, c)
+        gather(last, 3, 0, CHUNK)
+        gather(last, 3, CHUNK, tail)
+        for c in range(3):
+            interleave(last, c * CHUNK, (c + 1) * CHUNK)
+        gather(last, 0, tail, S)
+        quantize(last, 0, CHUNK)
+        multiply(last, 0)
+        gather(last, 1, tail, S)
+        quantize(last, CHUNK, HALF)
+        multiply(last, 1)
+        gather(last, 2, tail, S)
+        gather(last, 3, tail, S)
+        for n in range(N_TILES):
+            finish_on_scalar(0, n)
+        quantize(last, HALF, tail)
+        multiply(last, 2)
+        nc.vector.tensor_copy(*interleave_views(last, tail, S))
+        quantize(last, tail, S)
+        multiply(last, 3)
+        finish_on_scalar(1, 0)
+        finish_on_vector(1, 1)
+        finish_on_scalar(1, 2)
+        finish_on_vector(1, 3)

@@ -1,6 +1,7 @@
 from contextlib import ExitStack
 
 import concourse.mybir as mybir
+from concourse.masks import make_identity
 
 K, M, T, S = 1536, 512, 1024, 512
 FLOPS = 2 * K * M * S
@@ -25,7 +26,6 @@ LANES = 16
 CHUNK = 128
 HALF = 256
 N_TILES = M // P
-BIAS_PAD = 8
 
 
 def tile_list_heads_bias_kernel(tc, xT, w_words, w_scales, wgt, b, offs, out):
@@ -41,11 +41,12 @@ def tile_list_heads_bias_kernel(tc, xT, w_words, w_scales, wgt, b, offs, out):
         ]
         picked = [keep.tile([P, PACK, S], F32, name="picked_%d" % a) for a in range(PASSES)]
         grouped = [keep.tile([P, S, PACK], BF16, name="grouped_%d" % a, align_bytes=64) for a in range(PASSES)]
-        x_codes = keep.tile([P, PASSES, S], U32, name="x_codes", align_bytes=64)
         x_scales = keep.tile([P, PASSES, S], U8, name="x_scales", align_bytes=64)
         w_codes = keep.tile([P, PASSES, 2 * M], U8, name="w_codes", align_bytes=64)
         w_scale_rows = keep.tile([P, PASSES, M], U8, name="w_scale_rows", align_bytes=64)
-        bias = keep.tile([P, N_TILES, BIAS_PAD], F32, name="bias")
+        bias_rows = keep.tile([P, P], F32, name="bias_rows")
+        identity = keep.tile([P, P], F32, name="identity")
+        bias = keep.tile([P, N_TILES], F32, name="bias")
         result = keep.tile([P, S // HALF, N_TILES, HALF], F32, name="result")
         primer_in = keep.tile([P, 1], F32, name="primer_in")
         primer_out = keep.tile([P, 1], F32, name="primer_out")
@@ -55,11 +56,17 @@ def tile_list_heads_bias_kernel(tc, xT, w_words, w_scales, wgt, b, offs, out):
 
         nc.vector.memset(primer_in[:], 0.0)
         nc.scalar.activation(primer_out[:], primer_in[:], IDENTITY, bias=primer_in[:])
+        nc.vector.memset(bias_rows[:], 0.0)
         nc.vector.memset(w_scale_rows[:].bitcast(I32), 0)
+        make_identity(nc, identity[:])
 
         def load_plane(a, i):
             rows = xT[a * K_PASS : (a + 1) * K_PASS, :].rearrange("(p i) t -> p i t", i=PACK)
             nc.sync.dma_start(planes[a][i][:], rows[:, i, :])
+
+        def load_marker(a):
+            marker = keep.tile([LANES, 8], F32, name="marker_%d" % a, tag="x_codes_%d" % a, align_bytes=64)
+            nc.sync.dma_start(marker[:], wgt[0:LANES, 0:8])
 
         def load_w(a):
             nc.sync.dma_start(w_codes[:, a, :].bitcast(I32), w_words[a].bitcast(I32))
@@ -73,22 +80,30 @@ def tile_list_heads_bias_kernel(tc, xT, w_words, w_scales, wgt, b, offs, out):
 
         load_plane(0, 0)
         nc.sync.dma_start(offsets[:], offs)
-        nc.sync.dma_start(weights[:], wgt)
+        nc.sync.dma_start(weights[:, 0:CHUNK], wgt[:, 0:CHUNK])
+        nc.sync.dma_start(weights[:, CHUNK:S], wgt[:, CHUNK:S])
         for i in (1, 2, 3):
             load_plane(0, i)
-        for i in (0, 1):
+        nc.sync.dma_start(bias_rows[0:N_TILES, :], b.rearrange("(n p) -> n p", p=P))
+        for i in (0, 1, 2):
             load_plane(1, i)
-        load_w_scales()
-        for i in (2, 3):
-            load_plane(1, i)
-        load_w(0)
+        load_marker(0)
+        load_plane(1, 3)
         for i in (0, 1, 2):
             load_plane(2, i)
+        load_marker(1)
+        load_w_scales()
+        load_w(0)
         load_w(1)
         load_plane(2, 3)
         load_w(2)
-        with nc.allow_non_contiguous_dma(reason="one bias value to a partition"):
-            nc.sync.dma_start(bias[:, :, 0], b.rearrange("(n p) -> p n", p=P))
+
+        x_codes = [
+            keep.tile([P, S], U32, name="x_codes_%d" % a, tag="x_codes_%d" % a, align_bytes=64) for a in range(PASSES)
+        ]
+
+        nc.tensor.transpose(banks[1][0][:, 0:P], bias_rows[:], identity[:])
+        nc.scalar.copy(bias[:], banks[1][0][:, 0:N_TILES])
 
         def gather(a, i, lo, hi):
             window = planes[a][i][:].indirect(offsets[:, lo // LANES : hi // LANES])
@@ -104,7 +119,7 @@ def tile_list_heads_bias_kernel(tc, xT, w_words, w_scales, wgt, b, offs, out):
 
         def quantize(a, lo, hi):
             nc.vector.quantize_mx(
-                out=x_codes[:, a, lo:hi].bitcast(FP8X4),
+                out=x_codes[a][:, lo:hi].bitcast(FP8X4),
                 scales=x_scales[:, a, lo:hi],
                 in_=grouped[a][:, lo:hi, :].rearrange("p j i -> p (j i)"),
             )
@@ -117,7 +132,7 @@ def tile_list_heads_bias_kernel(tc, xT, w_words, w_scales, wgt, b, offs, out):
                     out=banks[h][n][:, side * CHUNK : (side + 1) * CHUNK],
                     lhsT=w_codes[:, a, 2 * P * n : 2 * P * (n + 1)].bitcast(FP4X4),
                     lhsT_scale=w_scale_rows[:, a, P * n : P * (n + 1)],
-                    rhs=x_codes[:, a, cols].bitcast(FP8X4),
+                    rhs=x_codes[a][:, cols].bitcast(FP8X4),
                     rhs_scale=x_scales[:, a, cols],
                     start=(a == 0 and side == 0),
                     stop=(a == PASSES - 1 and side == 1),
@@ -127,60 +142,50 @@ def tile_list_heads_bias_kernel(tc, xT, w_words, w_scales, wgt, b, offs, out):
             nc.sync.dma_start(out[P * n : P * (n + 1), HALF * h : HALF * (h + 1)], result[:, h, n, :])
 
         def finish_on_scalar(h, n):
-            nc.scalar.activation(result[:, h, n, :], banks[h][n][:], IDENTITY, bias=bias[:, n, 0:1])
+            nc.scalar.activation(result[:, h, n, :], banks[h][n][:], IDENTITY, bias=bias[:, n : n + 1])
             store(h, n)
 
         def finish_on_vector(h, n):
-            nc.vector.tensor_scalar(result[:, h, n, :], banks[h][n][:], bias[:, n, 0:1], None, ADD)
+            nc.vector.tensor_scalar(result[:, h, n, :], banks[h][n][:], bias[:, n : n + 1], None, ADD)
             store(h, n)
 
         def gather_in_halves(a, i):
             gather(a, i, 0, HALF)
             gather(a, i, HALF, S)
 
-        for i in range(PACK):
-            gather_in_halves(0, i)
-        interleave(0, 0, HALF)
-        interleave(0, HALF, S)
-        gather_in_halves(1, 0)
-        gather_in_halves(1, 1)
-        quantize(0, 0, S)
-        gather_in_halves(1, 2)
-        gather_in_halves(1, 3)
-        for c in range(4):
-            multiply(0, c)
-        interleave(1, 0, HALF)
-        interleave(1, HALF, S)
-
         last = PASSES - 1
-        tail = S - CHUNK
-        gather(last, 0, 0, tail)
-        gather(last, 1, 0, tail)
-        quantize(1, 0, HALF)
-        gather(last, 2, 0, tail)
-        quantize(1, HALF, S)
-        for c in range(4):
-            multiply(1, c)
-        gather(last, 3, 0, CHUNK)
-        gather(last, 3, CHUNK, tail)
-        for c in range(3):
-            interleave(last, c * CHUNK, (c + 1) * CHUNK)
-        gather(last, 0, tail, S)
-        quantize(last, 0, CHUNK)
-        multiply(last, 0)
-        gather(last, 1, tail, S)
-        quantize(last, CHUNK, HALF)
-        multiply(last, 1)
-        gather(last, 2, tail, S)
-        gather(last, 3, tail, S)
-        for n in range(N_TILES):
+        gather(0, 0, 0, CHUNK)
+        gather(0, 0, CHUNK, S)
+        for i in (1, 2, 3):
+            gather_in_halves(0, i)
+        for a in range(last):
+            interleave(a, 0, HALF)
+            interleave(a, HALF, S)
+            for i in (0, 1, 2):
+                gather_in_halves(a + 1, i)
+            quantize(a, 0, S)
+            for c in range(4):
+                multiply(a, c)
+            if a + 1 < last:
+                gather_in_halves(a + 1, 3)
+
+        chunk = [(c * CHUNK, (c + 1) * CHUNK) for c in range(4)]
+        gather(last, 3, *chunk[0])
+        gather(last, 3, *chunk[1])
+        gather(last, 3, HALF, S)
+        interleave(last, *chunk[0])
+        interleave(last, *chunk[2])
+        nc.vector.tensor_copy(*interleave_views(last, *chunk[1]))
+        for c in (0, 1):
+            quantize(last, *chunk[c])
+            multiply(last, c)
+        nc.vector.tensor_copy(*interleave_views(last, *chunk[3]))
+        for c in (2, 3):
+            quantize(last, *chunk[c])
+            multiply(last, c)
+        for n in range(3):
             finish_on_scalar(0, n)
-        quantize(last, HALF, tail)
-        multiply(last, 2)
-        nc.vector.tensor_copy(*interleave_views(last, tail, S))
-        quantize(last, tail, S)
-        multiply(last, 3)
-        finish_on_scalar(1, 0)
-        finish_on_vector(1, 1)
-        finish_on_scalar(1, 2)
-        finish_on_vector(1, 3)
+        finish_on_vector(0, 3)
+        for n in (0, 2):
+            finish_on_vector(1, n)
+            finish_on_scalar(1, n + 1)

@@ -25,6 +25,7 @@ PASSES = K // K_PASS
 LANES = 16
 CHUNK = 128
 HALF = 256
+WIDE = S - CHUNK
 N_TILES = M // P
 
 
@@ -36,10 +37,14 @@ def tile_list_heads_bias_kernel(tc, xT, w_words, w_scales, wgt, b, offs, out):
 
         offsets = keep.tile([P, S // LANES], U16, name="offsets")
         weights = keep.tile([P, S], F32, name="weights")
+        low_pair = keep.tile([P, 2, WIDE], F32, name="low_pair")
+        arena = keep.tile([P, 2 * WIDE + 2 * CHUNK], F32, name="arena")
+        high_pair = arena[:, 0 : 2 * WIDE].rearrange("p (i j) -> p i j", i=2)
+        last_tail = arena[:, PACK * CHUNK :].rearrange("p (i j) -> p i j", i=PACK)
         planes = [
             [keep.tile([P, T], F32, name="plane_%d_%d" % (a, i)) for i in range(PACK)] for a in range(PASSES)
         ]
-        picked = [keep.tile([P, PACK, S], F32, name="picked_%d" % a) for a in range(PASSES)]
+        picked = [keep.tile([P, PACK, S], F32, name="picked_%d" % a) for a in range(PASSES - 1)]
         grouped = [keep.tile([P, S, PACK], BF16, name="grouped_%d" % a, align_bytes=64) for a in range(PASSES)]
         x_scales = keep.tile([P, PASSES, S], U8, name="x_scales", align_bytes=64)
         w_codes = keep.tile([P, PASSES, 2 * M], U8, name="w_codes", align_bytes=64)
@@ -47,12 +52,11 @@ def tile_list_heads_bias_kernel(tc, xT, w_words, w_scales, wgt, b, offs, out):
         bias_rows = keep.tile([P, P], F32, name="bias_rows")
         identity = keep.tile([P, P], F32, name="identity")
         bias = keep.tile([P, N_TILES], F32, name="bias")
-        result = keep.tile([P, S // HALF, N_TILES, HALF], F32, name="result")
+        result = keep.tile([P, N_TILES, S], F32, name="result")
         primer_in = keep.tile([P, 1], F32, name="primer_in")
         primer_out = keep.tile([P, 1], F32, name="primer_out")
-        banks = [
-            [psum.tile([P, HALF], F32, name="bank_%d_%d" % (h, n)) for n in range(N_TILES)] for h in range(S // HALF)
-        ]
+        wide_banks = [psum.tile([P, WIDE], F32, name="wide_bank_%d" % n) for n in range(N_TILES)]
+        tail_banks = [psum.tile([P, CHUNK], F32, name="tail_bank_%d" % n) for n in range(N_TILES)]
 
         nc.vector.memset(primer_in[:], 0.0)
         nc.scalar.activation(primer_out[:], primer_in[:], IDENTITY, bias=primer_in[:])
@@ -89,10 +93,10 @@ def tile_list_heads_bias_kernel(tc, xT, w_words, w_scales, wgt, b, offs, out):
             load_plane(1, i)
         load_marker(0)
         load_plane(1, 3)
+        load_w_scales()
         for i in (0, 1, 2):
             load_plane(2, i)
         load_marker(1)
-        load_w_scales()
         load_w(0)
         load_w(1)
         load_plane(2, 3)
@@ -102,20 +106,20 @@ def tile_list_heads_bias_kernel(tc, xT, w_words, w_scales, wgt, b, offs, out):
             keep.tile([P, S], U32, name="x_codes_%d" % a, tag="x_codes_%d" % a, align_bytes=64) for a in range(PASSES)
         ]
 
-        nc.tensor.transpose(banks[1][0][:, 0:P], bias_rows[:], identity[:])
-        nc.scalar.copy(bias[:], banks[1][0][:, 0:N_TILES])
+        nc.tensor.transpose(tail_banks[0][:], bias_rows[:], identity[:])
+        nc.scalar.copy(bias[:], tail_banks[0][:, 0:N_TILES])
 
-        def gather(a, i, lo, hi):
+        last = PASSES - 1
+
+        def gather(a, i, lo, hi, dst):
             window = planes[a][i][:].indirect(offsets[:, lo // LANES : hi // LANES])
-            nc.vector.tensor_tensor(picked[a][:, i, lo:hi], window, weights[:, lo:hi], MULT)
+            nc.vector.tensor_tensor(dst, window, weights[:, lo:hi], MULT)
 
-        def interleave_views(a, lo, hi):
-            dst = grouped[a][:, lo:hi, :].rearrange("p (c e) i -> p c i e", e=4)
-            src = picked[a][:, :, lo:hi].rearrange("p i (c e) -> p c i e", e=4)
-            return dst, src
-
-        def interleave(a, lo, hi):
-            nc.scalar.copy(*interleave_views(a, lo, hi))
+        def interleave(copy, a, lo, hi, src, first=0, count=PACK):
+            copy(
+                grouped[a][:, lo:hi, first : first + count].rearrange("p (c e) i -> p c i e", e=4),
+                src.rearrange("p i (c e) -> p c i e", e=4),
+            )
 
         def quantize(a, lo, hi):
             nc.vector.quantize_mx(
@@ -125,67 +129,78 @@ def tile_list_heads_bias_kernel(tc, xT, w_words, w_scales, wgt, b, offs, out):
             )
 
         def multiply(a, c):
-            h, side = divmod(c, 2)
             cols = slice(c * CHUNK, (c + 1) * CHUNK)
+            in_tail = c == 3
             for n in range(N_TILES):
                 nc.tensor.matmul_mx(
-                    out=banks[h][n][:, side * CHUNK : (side + 1) * CHUNK],
+                    out=tail_banks[n][:] if in_tail else wide_banks[n][:, cols],
                     lhsT=w_codes[:, a, 2 * P * n : 2 * P * (n + 1)].bitcast(FP4X4),
                     lhsT_scale=w_scale_rows[:, a, P * n : P * (n + 1)],
                     rhs=x_codes[a][:, cols].bitcast(FP8X4),
                     rhs_scale=x_scales[:, a, cols],
-                    start=(a == 0 and side == 0),
-                    stop=(a == PASSES - 1 and side == 1),
+                    start=(a == 0 and c in (0, 3)),
+                    stop=(a == last and c in (2, 3)),
                 )
 
-        def store(h, n):
-            nc.sync.dma_start(out[P * n : P * (n + 1), HALF * h : HALF * (h + 1)], result[:, h, n, :])
+        out_rows = out.rearrange("(n p) j -> p n j", p=P)
 
-        def finish_on_scalar(h, n):
-            nc.scalar.activation(result[:, h, n, :], banks[h][n][:], IDENTITY, bias=bias[:, n : n + 1])
-            store(h, n)
+        def finish_on_scalar(n, bank, lo, hi):
+            nc.scalar.activation(result[:, n, lo:hi], bank[:], IDENTITY, bias=bias[:, n : n + 1])
 
-        def finish_on_vector(h, n):
-            nc.vector.tensor_scalar(result[:, h, n, :], banks[h][n][:], bias[:, n : n + 1], None, ADD)
-            store(h, n)
+        def finish_on_vector(n, bank, lo, hi):
+            nc.vector.tensor_scalar(result[:, n, lo:hi], bank[:], bias[:, n : n + 1], None, ADD)
 
-        def gather_in_halves(a, i):
-            gather(a, i, 0, HALF)
-            gather(a, i, HALF, S)
+        def store(first, count, lo, hi):
+            nc.sync.dma_start(out_rows[:, first : first + count, lo:hi], result[:, first : first + count, lo:hi])
 
-        last = PASSES - 1
-        gather(0, 0, 0, CHUNK)
-        gather(0, 0, CHUNK, S)
-        for i in (1, 2, 3):
-            gather_in_halves(0, i)
-        for a in range(last):
-            interleave(a, 0, HALF)
-            interleave(a, HALF, S)
-            for i in (0, 1, 2):
-                gather_in_halves(a + 1, i)
+        def gather_plane(a, i, cut):
+            gather(a, i, 0, cut, picked[a][:, i, 0:cut])
+            gather(a, i, cut, S, picked[a][:, i, cut:S])
+
+        def finish_pass(a):
             quantize(a, 0, S)
             for c in range(4):
                 multiply(a, c)
-            if a + 1 < last:
-                gather_in_halves(a + 1, 3)
 
-        chunk = [(c * CHUNK, (c + 1) * CHUNK) for c in range(4)]
-        gather(last, 3, *chunk[0])
-        gather(last, 3, *chunk[1])
-        gather(last, 3, HALF, S)
-        interleave(last, *chunk[0])
-        interleave(last, *chunk[2])
-        nc.vector.tensor_copy(*interleave_views(last, *chunk[1]))
-        for c in (0, 1):
-            quantize(last, *chunk[c])
+        def interleave_pass(a):
+            for lo in (0, HALF):
+                interleave(nc.scalar.copy, a, lo, lo + HALF, picked[a][:, :, lo : lo + HALF])
+
+        gather_plane(0, 0, CHUNK)
+        for i in (1, 2, 3):
+            gather_plane(0, i, HALF)
+        interleave_pass(0)
+        for i in (0, 1, 2):
+            gather_plane(1, i, HALF)
+        finish_pass(0)
+        gather_plane(1, 3, HALF)
+        interleave_pass(1)
+        for i in (0, 1):
+            gather(last, i, 0, WIDE, low_pair[:, i, :])
+        interleave(nc.scalar.copy, last, 0, WIDE, low_pair[:], 0, 2)
+        gather(last, 2, 0, WIDE, high_pair[:, 0, :])
+        gather(last, 2, WIDE, S, last_tail[:, 2, :])
+        finish_pass(1)
+
+        gather(last, 3, 0, CHUNK, high_pair[:, 1, 0:CHUNK])
+        gather(last, 3, CHUNK, WIDE, high_pair[:, 1, CHUNK:WIDE])
+        gather(last, 3, WIDE, S, last_tail[:, 3, :])
+        for c in range(3):
+            lo, hi = c * CHUNK, (c + 1) * CHUNK
+            interleave(nc.scalar.copy, last, lo, hi, high_pair[:, :, lo:hi], 2, 2)
+            quantize(last, lo, hi)
             multiply(last, c)
-        nc.vector.tensor_copy(*interleave_views(last, *chunk[3]))
-        for c in (2, 3):
-            quantize(last, *chunk[c])
-            multiply(last, c)
-        for n in range(3):
-            finish_on_scalar(0, n)
-        finish_on_vector(0, 3)
+            if c > 0:
+                gather(last, c - 1, WIDE, S, last_tail[:, c - 1, :])
+        for n in range(N_TILES - 1):
+            finish_on_scalar(n, wide_banks[n], 0, WIDE)
+            store(n, 1, 0, WIDE)
+        interleave(nc.vector.tensor_copy, last, WIDE, S, last_tail)
+        quantize(last, WIDE, S)
+        multiply(last, 3)
+        finish_on_vector(N_TILES - 1, wide_banks[N_TILES - 1], 0, WIDE)
+        store(N_TILES - 1, 1, 0, WIDE)
         for n in (0, 2):
-            finish_on_vector(1, n)
-            finish_on_scalar(1, n + 1)
+            finish_on_vector(n, tail_banks[n], WIDE, S)
+            finish_on_scalar(n + 1, tail_banks[n + 1], WIDE, S)
+            store(n, 2, WIDE, S)

from contextlib import ExitStack

import concourse.mybir as mybir
from concourse.masks import make_identity

K, M, T, S = 1536, 512, 1024, 512
FLOPS = 2 * K * M * S

F32 = mybir.dt.float32
BF16 = mybir.dt.bfloat16
I32 = mybir.dt.int32
U32 = mybir.dt.uint32
U16 = mybir.dt.uint16
U8 = mybir.dt.uint8
FP8X4 = mybir.dt.float8_e4m3fn_x4
FP4X4 = mybir.dt.float4_e2m1fn_x4
MULT = mybir.AluOpType.mult
ADD = mybir.AluOpType.add
IDENTITY = mybir.ActivationFunctionType.Identity

P = 128
PACK = 4
K_PASS = P * PACK
PASSES = K // K_PASS
LANES = 16
CHUNK = 128
HALF = 256
WIDE = S - CHUNK
N_TILES = M // P


def tile_list_heads_bias_kernel(tc, xT, w_words, w_scales, wgt, b, offs, out):
    nc = tc.nc
    with ExitStack() as ctx:
        keep = ctx.enter_context(tc.tile_pool(name="keep", bufs=1))
        psum = ctx.enter_context(tc.psum_pool(name="psum", bufs=1))

        offsets = keep.tile([P, S // LANES], U16, name="offsets")
        weights = keep.tile([P, S], F32, name="weights")
        low_pair = keep.tile([P, 2, WIDE], F32, name="low_pair")
        arena = keep.tile([P, 2 * WIDE + 2 * CHUNK], F32, name="arena")
        high_pair = arena[:, 0 : 2 * WIDE].rearrange("p (i j) -> p i j", i=2)
        last_tail = arena[:, PACK * CHUNK :].rearrange("p (i j) -> p i j", i=PACK)
        planes = [
            [keep.tile([P, T], F32, name="plane_%d_%d" % (a, i)) for i in range(PACK)] for a in range(PASSES)
        ]
        picked = [keep.tile([P, PACK, S], F32, name="picked_%d" % a) for a in range(PASSES - 1)]
        grouped = [keep.tile([P, S, PACK], BF16, name="grouped_%d" % a, align_bytes=64) for a in range(PASSES)]
        x_scales = keep.tile([P, PASSES, S], U8, name="x_scales", align_bytes=64)
        w_codes = keep.tile([P, PASSES, 2 * M], U8, name="w_codes", align_bytes=64)
        w_scale_rows = keep.tile([P, PASSES, M], U8, name="w_scale_rows", align_bytes=64)
        bias_rows = keep.tile([P, P], F32, name="bias_rows")
        identity = keep.tile([P, P], F32, name="identity")
        bias = keep.tile([P, N_TILES], F32, name="bias")
        result = keep.tile([P, N_TILES, S], F32, name="result")
        primer_in = keep.tile([P, 1], F32, name="primer_in")
        primer_out = keep.tile([P, 1], F32, name="primer_out")
        wide_banks = [psum.tile([P, WIDE], F32, name="wide_bank_%d" % n) for n in range(N_TILES)]
        tail_banks = [psum.tile([P, CHUNK], F32, name="tail_bank_%d" % n) for n in range(N_TILES)]

        nc.vector.memset(primer_in[:], 0.0)
        nc.scalar.activation(primer_out[:], primer_in[:], IDENTITY, bias=primer_in[:])
        nc.vector.memset(bias_rows[:], 0.0)
        nc.vector.memset(w_scale_rows[:].bitcast(I32), 0)
        make_identity(nc, identity[:])

        def load_plane(a, i):
            rows = xT[a * K_PASS : (a + 1) * K_PASS, :].rearrange("(p i) t -> p i t", i=PACK)
            nc.sync.dma_start(planes[a][i][:], rows[:, i, :])

        def load_marker(a):
            marker = keep.tile([LANES, 8], F32, name="marker_%d" % a, tag="x_codes_%d" % a, align_bytes=64)
            nc.sync.dma_start(marker[:], wgt[0:LANES, 0:8])

        def load_w(a):
            nc.sync.dma_start(w_codes[:, a, :].bitcast(I32), w_words[a].bitcast(I32))

        def load_w_scales():
            for q in range(4):
                nc.sync.dma_start(
                    w_scale_rows[32 * q : 32 * q + 4, :, :].bitcast(I32),
                    w_scales[:, 4 * q : 4 * q + 4, :].rearrange("a r n -> r a n").bitcast(I32),
                )

        load_plane(0, 0)
        nc.sync.dma_start(offsets[:], offs)
        nc.sync.dma_start(weights[:, 0:CHUNK], wgt[:, 0:CHUNK])
        nc.sync.dma_start(weights[:, CHUNK:S], wgt[:, CHUNK:S])
        for i in (1, 2, 3):
            load_plane(0, i)
        nc.sync.dma_start(bias_rows[0:N_TILES, :], b.rearrange("(n p) -> n p", p=P))
        for i in (0, 1, 2):
            load_plane(1, i)
        load_marker(0)
        load_plane(1, 3)
        load_w_scales()
        for i in (0, 1, 2):
            load_plane(2, i)
        load_marker(1)
        load_w(0)
        load_w(1)
        load_plane(2, 3)
        load_w(2)

        x_codes = [
            keep.tile([P, S], U32, name="x_codes_%d" % a, tag="x_codes_%d" % a, align_bytes=64) for a in range(PASSES)
        ]

        nc.tensor.transpose(tail_banks[0][:], bias_rows[:], identity[:])
        nc.scalar.copy(bias[:], tail_banks[0][:, 0:N_TILES])

        last = PASSES - 1

        def gather(a, i, lo, hi, dst):
            window = planes[a][i][:].indirect(offsets[:, lo // LANES : hi // LANES])
            nc.vector.tensor_tensor(dst, window, weights[:, lo:hi], MULT)

        def interleave(copy, a, lo, hi, src, first=0, count=PACK):
            copy(
                grouped[a][:, lo:hi, first : first + count].rearrange("p (c e) i -> p c i e", e=4),
                src.rearrange("p i (c e) -> p c i e", e=4),
            )

        def quantize(a, lo, hi):
            nc.vector.quantize_mx(
                out=x_codes[a][:, lo:hi].bitcast(FP8X4),
                scales=x_scales[:, a, lo:hi],
                in_=grouped[a][:, lo:hi, :].rearrange("p j i -> p (j i)"),
            )

        def multiply(a, c):
            cols = slice(c * CHUNK, (c + 1) * CHUNK)
            in_tail = c == 3
            for n in range(N_TILES):
                nc.tensor.matmul_mx(
                    out=tail_banks[n][:] if in_tail else wide_banks[n][:, cols],
                    lhsT=w_codes[:, a, 2 * P * n : 2 * P * (n + 1)].bitcast(FP4X4),
                    lhsT_scale=w_scale_rows[:, a, P * n : P * (n + 1)],
                    rhs=x_codes[a][:, cols].bitcast(FP8X4),
                    rhs_scale=x_scales[:, a, cols],
                    start=(a == 0 and c in (0, 3)),
                    stop=(a == last and c in (2, 3)),
                )

        out_rows = out.rearrange("(n p) j -> p n j", p=P)

        def finish_on_scalar(n, bank, lo, hi):
            nc.scalar.activation(result[:, n, lo:hi], bank[:], IDENTITY, bias=bias[:, n : n + 1])

        def finish_on_vector(n, bank, lo, hi):
            nc.vector.tensor_scalar(result[:, n, lo:hi], bank[:], bias[:, n : n + 1], None, ADD)

        def store(first, count, lo, hi):
            nc.sync.dma_start(out_rows[:, first : first + count, lo:hi], result[:, first : first + count, lo:hi])

        def gather_plane(a, i, cut):
            gather(a, i, 0, cut, picked[a][:, i, 0:cut])
            gather(a, i, cut, S, picked[a][:, i, cut:S])

        def finish_pass(a):
            quantize(a, 0, S)
            for c in range(4):
                multiply(a, c)

        def interleave_pass(a):
            for lo in (0, HALF):
                interleave(nc.scalar.copy, a, lo, lo + HALF, picked[a][:, :, lo : lo + HALF])

        gather_plane(0, 0, CHUNK)
        for i in (1, 2, 3):
            gather_plane(0, i, HALF)
        interleave_pass(0)
        for i in (0, 1, 2):
            gather_plane(1, i, HALF)
        finish_pass(0)
        gather_plane(1, 3, HALF)
        interleave_pass(1)
        for i in (0, 1):
            gather(last, i, 0, WIDE, low_pair[:, i, :])
        interleave(nc.scalar.copy, last, 0, WIDE, low_pair[:], 0, 2)
        gather(last, 2, 0, WIDE, high_pair[:, 0, :])
        gather(last, 2, WIDE, S, last_tail[:, 2, :])
        finish_pass(1)

        gather(last, 3, 0, CHUNK, high_pair[:, 1, 0:CHUNK])
        gather(last, 3, CHUNK, WIDE, high_pair[:, 1, CHUNK:WIDE])
        gather(last, 3, WIDE, S, last_tail[:, 3, :])
        for c in range(3):
            lo, hi = c * CHUNK, (c + 1) * CHUNK
            interleave(nc.scalar.copy, last, lo, hi, high_pair[:, :, lo:hi], 2, 2)
            quantize(last, lo, hi)
            multiply(last, c)
            if c > 0:
                gather(last, c - 1, WIDE, S, last_tail[:, c - 1, :])
        for n in range(N_TILES - 1):
            finish_on_scalar(n, wide_banks[n], 0, WIDE)
            store(n, 1, 0, WIDE)
        interleave(nc.vector.tensor_copy, last, WIDE, S, last_tail)
        quantize(last, WIDE, S)
        multiply(last, 3)
        finish_on_vector(N_TILES - 1, wide_banks[N_TILES - 1], 0, WIDE)
        store(N_TILES - 1, 1, 0, WIDE)
        for n in (0, 2):
            finish_on_vector(n, tail_banks[n], WIDE, S)
            finish_on_scalar(n + 1, tail_banks[n + 1], WIDE, S)
            store(n, 2, WIDE, S)
